import numpy as np
import ml_dtypes


def mxq(x, axis, fmt="e4m3"):
    dtype, down = {"e4m3": (ml_dtypes.float8_e4m3fn, 7), "e5m2": (ml_dtypes.float8_e5m2, 14)}[fmt]
    v = np.moveaxis(np.asarray(x, np.float32).astype(ml_dtypes.bfloat16).astype(np.float64), axis, -1)
    blocks = v.reshape(v.shape[:-1] + (-1, 32))
    amax = np.abs(blocks).max(-1, keepdims=True)
    byte = np.maximum(np.where(amax > 0, np.frexp(amax)[1] - 1 + 127, 0) - down, 1)
    scale = np.exp2(byte - 127.0)
    codes = (blocks / scale).astype(np.float32).astype(dtype).astype(np.float64)
    return np.moveaxis((codes * scale).reshape(v.shape), -1, axis)


WIDE = False


def mx_kscale(k):
    if not WIDE:
        return np.ones(k)
    levels = np.array([10, -10, 5, -5, 0])
    if k % 512:
        return np.exp2(np.random.permutation(np.resize(levels, k // 32))).repeat(32)
    a = np.empty((k // 512, 16))
    for p in range(k // 512):
        a[p, :8] = np.random.permutation(np.resize(levels, 8))
        for g in range(8):
            far = levels[np.abs(levels - a[p, g]) >= 10]
            a[p, g + 8] = far[np.random.randint(len(far))]
    return np.exp2(a.ravel()).repeat(32)


def f64(x):
    return np.asarray(x).astype(np.float64)


def striped(idx):
    return np.tile(np.asarray(idx).reshape(-1, 16).T, (8, 1)).astype(np.uint16)


def unstriped(offs):
    return offs[:16].T.reshape(-1).astype(np.int64)


E2M1 = np.array([0.0, 0.5, 1.0, 1.5, 2.0, 3.0, 4.0, 6.0, -0.0, -0.5, -1.0, -1.5, -2.0, -3.0, -4.0, -6.0])


def pack_weight(w, fmt):
    k, n = w.shape
    w = f64(np.asarray(w, np.float32).astype(ml_dtypes.bfloat16)).reshape(k // 32, 32, n)
    amax = np.abs(w).max(1)
    if fmt == "e4m3":
        byte = np.frexp(amax)[1] - 1 + 127 - 7
    else:
        mant, ex = np.frexp(amax / 6.0)
        byte = np.where(mant > 0.5, ex, ex - 1) + 127
    byte = np.clip(np.where(amax > 0, byte, 1), 1, 254)
    scaled = (w * np.exp2(127.0 - byte)[:, None, :]).reshape(k, n).astype(np.float32)
    by_word = np.ascontiguousarray(scaled.reshape(k // 512, 128, 4, n).transpose(0, 1, 3, 2))
    if fmt == "e4m3":
        words = by_word.astype(ml_dtypes.float8_e4m3fn).view(np.uint8)
    else:
        c = by_word.astype(ml_dtypes.float4_e2m1fn).view(np.uint8) & 0xF
        words = (c[..., 0::2] | (c[..., 1::2] << 4)).reshape(k // 512, 128, 2 * n)
    return np.ascontiguousarray(words), np.ascontiguousarray(byte.astype(np.uint8).reshape(k // 512, 16, n))


def unpack_weight(words, scales, fmt):
    g, _, n = scales.shape
    words = np.ascontiguousarray(words).reshape(g, 128, n, -1)
    if fmt == "e4m3":
        vals = words.view(ml_dtypes.float8_e4m3fn).astype(np.float64)
    else:
        nib = np.empty((g, 128, n, 4), np.uint8)
        nib[..., 0::2] = words & 0xF
        nib[..., 1::2] = words >> 4
        vals = E2M1[nib]
    vals = vals * np.repeat(np.exp2(scales.astype(np.float64) - 127.0), 8, axis=1)[..., None]
    return vals.transpose(0, 1, 3, 2).reshape(g * 512, n)


D, T, I, J, U, E, C = 512, 2048, 512, 512, 1024, 512, 256


def setup_inputs():
    n = np.random.standard_normal
    idx = np.random.permutation(T)[:I]
    idx2 = np.random.permutation(U)[:J]
    idx3 = np.random.permutation(J)[:C]
    fd = mx_kscale(D)
    fi = mx_kscale(I)
    ti = np.ones(T)
    ti[idx] = fi
    keysp = pack_weight(n((D, T)) / fd[:, None], "e4m3")
    return {
        "keys_words": keysp[0],
        "keys_scales": keysp[1],
        "notes": (n((D, U)) * 1.0 / np.sqrt(D) * fd[:, None]).astype(np.float32),
        "rowf": (np.random.uniform(0.02, 0.08, (I, 1)) * fi[:, None]).astype(np.float32),
        "vals": (n((E, T)) / ti).astype(np.float32),
        "pgain": (np.random.uniform(0.5, 2.0, (1, C))).astype(np.float32),
        "offs": striped(idx),
        "offs2": striped(idx2),
        "offs3": striped(idx3),
    }


def reference(keys_words, keys_scales, notes, rowf, vals, pgain, offs, offs2, offs3):
    idx = unstriped(offs)
    idx2 = unstriped(offs2)
    idx3 = unstriped(offs3)
    keysu = unpack_weight(keys_words, keys_scales, "e4m3")
    keysidxg = keysu[:, idx]
    notesidx2q = mxq(f64(notes)[:, idx2], 0, "e4m3")
    g9 = keysidxg.T @ notesidx2q
    g0 = np.maximum(g9, 0.0)
    gr1 = g0 * f64(rowf)
    vt1 = f64(vals)[:, idx].T
    vt1q = mxq(vt1, 0, "e4m3")
    gr1q = mxq(gr1, 0, "e4m3")
    o = vt1q.T @ gr1q
    y = o[:, idx3] * f64(pgain)
    return y

@@ -1,0 +1,229 @@
+from contextlib import ExitStack
+
+import concourse.mybir as mybir
+from concourse.masks import make_identity
+
+D, T, I, J, U, E, C = 512, 2048, 512, 512, 1024, 512, 256
+FLOPS = 2 * D * I * J + 2 * I * E * J
+
+F32 = mybir.dt.float32
+BF16 = mybir.dt.bfloat16
+I32 = mybir.dt.int32
+U32 = mybir.dt.uint32
+U16 = mybir.dt.uint16
+U8 = mybir.dt.uint8
+FP8X4 = mybir.dt.float8_e4m3fn_x4
+COPY = mybir.ActivationFunctionType.Copy
+MULT = mybir.AluOpType.mult
+MAX = mybir.AluOpType.max
+
+P = 128
+PACK = 4
+NOTES_AT = 12288
+WOVEN_AT = 8192
+THIRD_AT = 16384
+LAST_SPLIT = 320
+
+
+def tile_attend_tab_plain_picked_kernel(tc, keys_words, keys_scales, notes, rowf, vals, pgain, offs, offs2, offs3, out):
+    nc = tc.nc
+    with ExitStack() as ctx:
+        sb = ctx.enter_context(tc.tile_pool(name="sb", bufs=1))
+        last = ctx.enter_context(tc.tile_pool(name="last", bufs=1))
+        psum = ctx.enter_context(tc.psum_pool(name="psum", bufs=1))
+
+        token_list = sb.tile([P, I // 16], U16)
+        note_list = sb.tile([P, J // 16], U16)
+        column_list = sb.tile([P, C // 16], U16)
+        key_pool = sb.tile([P, T], U32, tag="key_pool", align_bytes=64)
+        scale_rows = sb.tile([P, 2, T], U8)
+        scale_pool = sb.tile([P, T], U8)
+        note_pool = [sb.tile([P, U], F32, name="note_pool%d" % t) for t in range(PACK)]
+        value_pool = [sb.tile([P, T], F32, name="value_pool%d" % b) for b in range(2)]
+        value_pool.append(last.tile([P, T], F32, name="value_pool2", offset=THIRD_AT))
+        value_pool.append(last.tile([P, T], F32, name="value_pool3", offset=0))
+        row_factor = sb.tile([P, PACK], F32)
+        gain_pairs = last.tile([P, 2], F32, offset=NOTES_AT)
+        identity = sb.tile([P, P], F32)
+
+        make_identity(nc, identity[:])
+        nc.vector.memset(scale_pool[:].bitcast(I32), 0)
+
+        note_planes = notes.rearrange("(p t) u -> p t u", t=PACK)
+        nc.sync.dma_start(gain_pairs[:], pgain.rearrange("o (p t) -> (o p) t", t=2))
+        nc.sync.dma_start(note_pool[0][:], note_planes[:, 0, :])
+        for h in range(2):
+            nc.scalar.dma_start(
+                scale_rows[64 * h : 64 * h + 4, :, :].bitcast(I32),
+                keys_scales[0, 8 * h : 8 * h + 8, :].rearrange("(q r) c -> r q c", r=4).bitcast(I32),
+            )
+        nc.sync.dma_start(note_list[:], offs2)
+        nc.sync.dma_start(token_list[:], offs)
+        for t in range(1, PACK):
+            nc.sync.dma_start(note_pool[t][:], note_planes[:, t, :])
+        nc.sync.dma_start(key_pool[:].bitcast(I32), keys_words[0].rearrange("p n t -> p (n t)").bitcast(I32))
+        nc.sync.dma_start(row_factor[:], rowf.rearrange("(p t) o -> p (t o)", t=PACK))
+        nc.sync.dma_start(value_pool[0][:], vals[0:P, :])
+        nc.sync.dma_start(column_list[:], offs3)
+        for b in range(1, E // P):
+            nc.sync.dma_start(value_pool[b][:], vals[b * P : (b + 1) * P, :])
+
+        gain_ps = psum.tile([P, 2, P], F32, tag="bank_d", bufs=1)
+        for t in range(2):
+            nc.tensor.transpose(gain_ps[:, t, :], gain_pairs[:, t : t + 1].to_broadcast([P, P]), identity[:])
+        gain = sb.tile([P, C], F32)
+        nc.scalar.copy(gain[:].rearrange("p (k t) -> p k t", t=2), gain_ps[:].rearrange("p t k -> p k t"))
+
+        for q in range(4):
+            h, g = divmod(q, 2)
+            nc.vector.tensor_copy(
+                scale_pool[32 * q : 32 * q + 4, :].bitcast(I32), scale_rows[64 * h : 64 * h + 4, g, :].bitcast(I32)
+            )
+        key_scales = sb.tile([P, I], U8, align_bytes=64)
+        nc.vector.tensor_copy(
+            key_scales[:].rearrange("p (r s) -> p s r", r=PACK), scale_pool[:].indirect(token_list[:])
+        )
+
+        note_picked = last.tile([P, PACK, J], BF16, offset=NOTES_AT)
+        for t in range(2):
+            nc.scalar.activation(note_picked[:, t, :], note_pool[t][:].indirect(note_list[:]), COPY)
+        nc.vector.tensor_copy(note_picked[:, 2, :], note_pool[2][:].indirect(note_list[:]))
+        half = J // 2
+        note_woven = [sb.tile([P, half, PACK], BF16, name="note_woven%d" % h, tag="note_woven%d" % h, align_bytes=64) for h in range(2)]
+        nc.vector.tensor_copy(note_picked[:, 3, :half], note_pool[3][:].indirect(note_list[:, : half // 16]))
+        nc.scalar.activation(note_picked[:, 3, half:], note_pool[3][:].indirect(note_list[:, half // 16 :]), COPY)
+        nc.vector.tensor_copy(
+            note_woven[0][:].rearrange("p (c i) t -> p c t i", i=4),
+            note_picked[:, :, :half].rearrange("p t (c i) -> p c t i", i=4),
+        )
+        nc.scalar.copy(
+            note_woven[1][:].rearrange("p (c i) t -> p c t i", i=4),
+            note_picked[:, :, half:].rearrange("p t (c i) -> p c t i", i=4),
+        )
+        note_scales = [sb.tile([P, half], U8, name="note_scales%d" % h, align_bytes=64) for h in range(2)]
+        note_codes = [sb.tile([P, half], U32, name="note_codes0", align_bytes=64)]
+        nc.vector.quantize_mx(
+            out=note_codes[0][:].bitcast(FP8X4), scales=note_scales[0][:], in_=note_woven[0][:].rearrange("p j t -> p (j t)")
+        )
+        key_codes = sb.tile([P, I], U32, tag="note_woven0", align_bytes=64)
+        nc.vector.tensor_copy(key_codes[:].rearrange("p (r s) -> p s r", r=PACK), key_pool[:].indirect(token_list[:]))
+        note_codes.append(sb.tile([P, half], U32, name="note_codes1", tag="key_pool", align_bytes=64))
+        nc.vector.quantize_mx(
+            out=note_codes[1][:].bitcast(FP8X4), scales=note_scales[1][:], in_=note_woven[1][:].rearrange("p j t -> p (j t)")
+        )
+
+        table = sb.tile([P, J, PACK], BF16, tag="table", align_bytes=64)
+        for q in range(J // P):
+            cols = slice(q * P, (q + 1) * P)
+            h, within = q // 2, slice(q % 2 * P, (q % 2 + 1) * P)
+            raw = psum.tile([P, PACK, P], F32, tag="raw", bufs=4)
+            for r in range(PACK):
+                rows = slice(r * P, (r + 1) * P)
+                nc.tensor.matmul_mx(
+                    out=raw[:, r, :],
+                    lhsT=key_codes[:, rows].bitcast(FP8X4),
+                    lhsT_scale=key_scales[:, rows],
+                    rhs=note_codes[h][:, within].bitcast(FP8X4),
+                    rhs_scale=note_scales[h][:, within],
+                    start=True,
+                    stop=True,
+                )
+            nc.vector.scalar_tensor_tensor(
+                out=table[:, cols, :],
+                in0=raw[:].rearrange("p r j -> p j r"),
+                scalar=0.0,
+                in1=row_factor[:].unsqueeze(1).to_broadcast([P, P, PACK]),
+                op0=MAX,
+                op1=MULT,
+            )
+        table_codes = sb.tile([P, J], U32, align_bytes=64)
+        table_scales = sb.tile([P, J], U8, align_bytes=64)
+        for cols in (slice(0, J // 2), slice(J // 2, J)):
+            nc.vector.quantize_mx(
+                out=table_codes[:, cols].bitcast(FP8X4),
+                scales=table_scales[:, cols],
+                in_=table[:, cols, :].rearrange("p j r -> p (j r)"),
+            )
+
+        value_woven, value_codes, value_scales, whole, banks, turned_banks = {}, {}, {}, {}, {}, {}
+
+        def turn(b, picked, turned, scalar_share):
+            cut = scalar_share // 16
+            if scalar_share > 0:
+                nc.scalar.activation(picked[:, :scalar_share], value_pool[b][:].indirect(token_list[:, :cut]), COPY)
+            if scalar_share < I:
+                nc.vector.tensor_copy(picked[:, scalar_share:], value_pool[b][:].indirect(token_list[:, cut:]))
+            pairs = picked[:].bitcast(F32)
+            for u in range(2):
+                nc.tensor.transpose(turned[:, u, :], pairs[:, u : I // 2 : 2], identity[:])
+            turned_banks[b] = turned
+
+        def weave(b, woven):
+            value_woven[b] = woven
+            nc.scalar.copy(
+                woven[:].bitcast(F32).rearrange("p (e u) -> p e u", u=2), turned_banks[b][:].rearrange("p u e -> p e u")
+            )
+
+        def quantise(b, codes):
+            value_codes[b] = codes
+            value_scales[b] = sb.tile([P, P], U8, name="value_scales%d" % b, align_bytes=64)
+            nc.vector.quantize_mx(out=codes[:].bitcast(FP8X4), scales=value_scales[b][:], in_=value_woven[b][:])
+
+        def multiply(b, bank, window):
+            sums = psum.tile([P, J], F32, name="sums", tag=bank, bufs=1)
+            nc.tensor.matmul_mx(
+                out=sums[:],
+                lhsT=value_codes[b][:].bitcast(FP8X4),
+                lhsT_scale=value_scales[b][:],
+                rhs=table_codes[:].bitcast(FP8X4),
+                rhs_scale=table_scales[:],
+                start=True,
+                stop=True,
+            )
+            banks[b] = sums
+            if window is not None:
+                copy_out(b, window)
+
+        def copy_out(b, window):
+            whole[b] = window
+            if b == 0:
+                nc.vector.tensor_copy(window[:], banks[b][:])
+            else:
+                nc.scalar.copy(window[:], banks[b][:])
+
+        def give_out(b, result):
+            nc.vector.tensor_tensor(result[:], whole[b][:].indirect(column_list[:]), gain[:], MULT)
+            nc.sync.dma_start(out[b * P : (b + 1) * P, :], result[:])
+
+        def turned_on(tag, bufs):
+            return psum.tile([P, 2, P], F32, name="turned", tag=tag, bufs=bufs)
+
+        def woven_on(b):
+            return sb.tile([P, P * PACK], BF16, name="woven%d" % b, tag="woven%d" % b, align_bytes=64)
+
+        def codes_on(b, tag):
+            return sb.tile([P, P], U32, name="value_codes%d" % b, tag=tag, align_bytes=64)
+
+
+        turn(0, last.tile([P, I], BF16, name="picked0", offset=NOTES_AT), turned_on("raw", 4), I)
+        weave(0, woven_on(0))
+        quantise(0, codes_on(0, "table"))
+        multiply(0, "bank_a", None)
+        turn(1, sb.tile([P, I], BF16, name="picked1"), turned_on("bank_b", 1), I)
+        turn(2, sb.tile([P, I], BF16, name="picked2", tag="woven0", align_bytes=64), turned_on("bank_c", 1), I // 2)
+        weave(1, last.tile([P, P * PACK], BF16, name="woven1", offset=THIRD_AT + 4096, align_bytes=64))
+        weave(2, woven_on(2))
+        copy_out(0, last.tile([P, J], F32, name="whole0", offset=THIRD_AT))
+        quantise(1, last.tile([P, P], U32, name="value_codes1", offset=THIRD_AT + 2048, align_bytes=64))
+        give_out(0, sb.tile([P, C], F32, name="result0"))
+        multiply(1, "bank_b", None)
+        turn(3, sb.tile([P, I], BF16, name="picked3", tag="woven0", align_bytes=64), turned_on("bank_c", 1), LAST_SPLIT)
+        copy_out(1, last.tile([P, J], F32, name="whole1", offset=0))
+        weave(3, last.tile([P, P * PACK], BF16, name="woven3", offset=WOVEN_AT + 1536, align_bytes=64))
+        quantise(2, last.tile([P, P], U32, name="value_codes2", offset=2048, align_bytes=64))
+        quantise(3, codes_on(3, "value_codes3"))
+        multiply(2, "bank_a", last.tile([P, J], F32, name="whole2", offset=WOVEN_AT))
+        multiply(3, "bank_d", sb.tile([P, J], F32, name="whole3"))
+        give_out(1, last.tile([P, C], F32, name="result1", offset=WOVEN_AT + 2048))
+        give_out(2, sb.tile([P, C], F32, name="result2"))
+        give_out(3, sb.tile([P, C], F32, name="result3"))

@@ -19,31 +19,45 @@ MAX = mybir.AluOpType.max
 
 P = 128
 PACK = 4
-NOTES_AT = 12288
-WOVEN_AT = 8192
-THIRD_AT = 16384
-LAST_SPLIT = 320
+GROUP = 16
+MX_ALIGN = 64
+HALF = 256
+RAW_BANKS = J // P
 
 
 def tile_attend_tab_plain_picked_kernel(tc, keys_words, keys_scales, notes, rowf, vals, pgain, offs, offs2, offs3, out):
     nc = tc.nc
     with ExitStack() as ctx:
         sb = ctx.enter_context(tc.tile_pool(name="sb", bufs=1))
-        last = ctx.enter_context(tc.tile_pool(name="last", bufs=1))
         psum = ctx.enter_context(tc.psum_pool(name="psum", bufs=1))
 
-        token_list = sb.tile([P, I // 16], U16)
-        note_list = sb.tile([P, J // 16], U16)
-        column_list = sb.tile([P, C // 16], U16)
-        key_pool = sb.tile([P, T], U32, tag="key_pool", align_bytes=64)
+        def on_buffer(shape, dtype, name, tag):
+            return sb.tile(shape, dtype, name=name, tag=tag, align_bytes=MX_ALIGN)
+
+        def quantise(codes, scales, woven):
+            nc.vector.quantize_mx(out=codes.bitcast(FP8X4), scales=scales, in_=woven)
+
+        def product(sums, lhs_codes, lhs_scales, rhs_codes, rhs_scales):
+            nc.tensor.matmul_mx(
+                out=sums,
+                lhsT=lhs_codes.bitcast(FP8X4),
+                lhsT_scale=lhs_scales,
+                rhs=rhs_codes.bitcast(FP8X4),
+                rhs_scale=rhs_scales,
+                start=True,
+                stop=True,
+            )
+
+        token_list = sb.tile([P, I // GROUP], U16)
+        note_list = sb.tile([P, J // GROUP], U16)
+        column_list = sb.tile([P, C // GROUP], U16)
+        key_pool = on_buffer([P, T], U32, "key_pool", "key_pool")
         scale_rows = sb.tile([P, 2, T], U8)
         scale_pool = sb.tile([P, T], U8)
         note_pool = [sb.tile([P, U], F32, name="note_pool%d" % t) for t in range(PACK)]
-        value_pool = [sb.tile([P, T], F32, name="value_pool%d" % b) for b in range(2)]
-        value_pool.append(last.tile([P, T], F32, name="value_pool2", offset=THIRD_AT))
-        value_pool.append(last.tile([P, T], F32, name="value_pool3", offset=0))
+        value_pool = [on_buffer([P, T], F32, "value_pool%d" % b, "value_pool%d" % b) for b in range(E // P)]
         row_factor = sb.tile([P, PACK], F32)
-        gain_pairs = last.tile([P, 2], F32, offset=NOTES_AT)
+        gain_pairs = on_buffer([P, 2], F32, "gain_pairs", "picked_first")
         identity = sb.tile([P, P], F32)
 
         make_identity(nc, identity[:])
@@ -68,162 +82,124 @@ def tile_attend_tab_plain_picked_kernel(tc, keys_words, keys_scales, notes, rowf
         for b in range(1, E // P):
             nc.sync.dma_start(value_pool[b][:], vals[b * P : (b + 1) * P, :])
 
-        gain_ps = psum.tile([P, 2, P], F32, tag="bank_d", bufs=1)
+        gain_turned = psum.tile([P, 2, P], F32, tag="turned", bufs=2)
         for t in range(2):
-            nc.tensor.transpose(gain_ps[:, t, :], gain_pairs[:, t : t + 1].to_broadcast([P, P]), identity[:])
+            nc.tensor.transpose(gain_turned[:, t, :], gain_pairs[:, t : t + 1].to_broadcast([P, P]), identity[:])
         gain = sb.tile([P, C], F32)
-        nc.scalar.copy(gain[:].rearrange("p (k t) -> p k t", t=2), gain_ps[:].rearrange("p t k -> p k t"))
+        nc.scalar.copy(gain[:].rearrange("p (k t) -> p k t", t=2), gain_turned[:].rearrange("p t k -> p k t"))
 
         for q in range(4):
-            h, g = divmod(q, 2)
+            h, pair = divmod(q, 2)
             nc.vector.tensor_copy(
-                scale_pool[32 * q : 32 * q + 4, :].bitcast(I32), scale_rows[64 * h : 64 * h + 4, g, :].bitcast(I32)
+                scale_pool[32 * q : 32 * q + 4, :].bitcast(I32), scale_rows[64 * h : 64 * h + 4, pair, :].bitcast(I32)
             )
-        key_scales = sb.tile([P, I], U8, align_bytes=64)
+        key_scales = sb.tile([P, I], U8, align_bytes=MX_ALIGN)
         nc.vector.tensor_copy(
             key_scales[:].rearrange("p (r s) -> p s r", r=PACK), scale_pool[:].indirect(token_list[:])
         )
 
-        note_picked = last.tile([P, PACK, J], BF16, offset=NOTES_AT)
+        note_picked = on_buffer([P, PACK, J], BF16, "note_picked", "picked_first")
         for t in range(2):
             nc.scalar.activation(note_picked[:, t, :], note_pool[t][:].indirect(note_list[:]), COPY)
         nc.vector.tensor_copy(note_picked[:, 2, :], note_pool[2][:].indirect(note_list[:]))
-        half = J // 2
-        note_woven = [sb.tile([P, half, PACK], BF16, name="note_woven%d" % h, tag="note_woven%d" % h, align_bytes=64) for h in range(2)]
-        nc.vector.tensor_copy(note_picked[:, 3, :half], note_pool[3][:].indirect(note_list[:, : half // 16]))
-        nc.scalar.activation(note_picked[:, 3, half:], note_pool[3][:].indirect(note_list[:, half // 16 :]), COPY)
-        nc.vector.tensor_copy(
-            note_woven[0][:].rearrange("p (c i) t -> p c t i", i=4),
-            note_picked[:, :, :half].rearrange("p t (c i) -> p c t i", i=4),
-        )
-        nc.scalar.copy(
-            note_woven[1][:].rearrange("p (c i) t -> p c t i", i=4),
-            note_picked[:, :, half:].rearrange("p t (c i) -> p c t i", i=4),
-        )
-        note_scales = [sb.tile([P, half], U8, name="note_scales%d" % h, align_bytes=64) for h in range(2)]
-        note_codes = [sb.tile([P, half], U32, name="note_codes0", align_bytes=64)]
-        nc.vector.quantize_mx(
-            out=note_codes[0][:].bitcast(FP8X4), scales=note_scales[0][:], in_=note_woven[0][:].rearrange("p j t -> p (j t)")
-        )
-        key_codes = sb.tile([P, I], U32, tag="note_woven0", align_bytes=64)
-        nc.vector.tensor_copy(key_codes[:].rearrange("p (r s) -> p s r", r=PACK), key_pool[:].indirect(token_list[:]))
-        note_codes.append(sb.tile([P, half], U32, name="note_codes1", tag="key_pool", align_bytes=64))
-        nc.vector.quantize_mx(
-            out=note_codes[1][:].bitcast(FP8X4), scales=note_scales[1][:], in_=note_woven[1][:].rearrange("p j t -> p (j t)")
-        )
+        nc.vector.tensor_copy(note_picked[:, 3, :HALF], note_pool[3][:].indirect(note_list[:, : HALF // GROUP]))
+        nc.scalar.activation(note_picked[:, 3, HALF:], note_pool[3][:].indirect(note_list[:, HALF // GROUP :]), COPY)
 
-        table = sb.tile([P, J, PACK], BF16, tag="table", align_bytes=64)
-        for q in range(J // P):
-            cols = slice(q * P, (q + 1) * P)
-            h, within = q // 2, slice(q % 2 * P, (q % 2 + 1) * P)
-            raw = psum.tile([P, PACK, P], F32, tag="raw", bufs=4)
+        note_woven = [on_buffer([P, HALF, PACK], BF16, "note_woven%d" % h, "note_woven%d" % h) for h in range(2)]
+        for h, copy in enumerate((nc.vector.tensor_copy, nc.scalar.copy)):
+            copy(
+                note_woven[h][:].rearrange("p (c i) t -> p c t i", i=4),
+                note_picked[:, :, h * HALF : (h + 1) * HALF].rearrange("p t (c i) -> p c t i", i=4),
+            )
+
+        note_scales = [sb.tile([P, HALF], U8, name="note_scales%d" % h, align_bytes=MX_ALIGN) for h in range(2)]
+        note_codes = [sb.tile([P, HALF], U32, name="note_codes0", align_bytes=MX_ALIGN)]
+        quantise(note_codes[0][:], note_scales[0][:], note_woven[0][:].rearrange("p j t -> p (j t)"))
+        key_codes = on_buffer([P, I], U32, "key_codes", "note_woven0")
+        nc.vector.tensor_copy(key_codes[:].rearrange("p (r s) -> p s r", r=PACK), key_pool[:].indirect(token_list[:]))
+        note_codes.append(on_buffer([P, HALF], U32, "note_codes1", "key_pool"))
+        quantise(note_codes[1][:], note_scales[1][:], note_woven[1][:].rearrange("p j t -> p (j t)"))
+
+        table = on_buffer([P, J, PACK], BF16, "table", "table")
+        for q in range(RAW_BANKS):
+            h, within = divmod(q * P, HALF)
+            cols = slice(within, within + P)
+            raw = psum.tile([P, PACK, P], F32, tag="raw", bufs=RAW_BANKS)
             for r in range(PACK):
                 rows = slice(r * P, (r + 1) * P)
-                nc.tensor.matmul_mx(
-                    out=raw[:, r, :],
-                    lhsT=key_codes[:, rows].bitcast(FP8X4),
-                    lhsT_scale=key_scales[:, rows],
-                    rhs=note_codes[h][:, within].bitcast(FP8X4),
-                    rhs_scale=note_scales[h][:, within],
-                    start=True,
-                    stop=True,
-                )
+                product(raw[:, r, :], key_codes[:, rows], key_scales[:, rows], note_codes[h][:, cols], note_scales[h][:, cols])
             nc.vector.scalar_tensor_tensor(
-                out=table[:, cols, :],
+                out=table[:, q * P : (q + 1) * P, :],
                 in0=raw[:].rearrange("p r j -> p j r"),
                 scalar=0.0,
                 in1=row_factor[:].unsqueeze(1).to_broadcast([P, P, PACK]),
                 op0=MAX,
                 op1=MULT,
             )
-        table_codes = sb.tile([P, J], U32, align_bytes=64)
-        table_scales = sb.tile([P, J], U8, align_bytes=64)
-        for cols in (slice(0, J // 2), slice(J // 2, J)):
-            nc.vector.quantize_mx(
-                out=table_codes[:, cols].bitcast(FP8X4),
-                scales=table_scales[:, cols],
-                in_=table[:, cols, :].rearrange("p j r -> p (j r)"),
-            )
+        table_codes = sb.tile([P, J], U32, align_bytes=MX_ALIGN)
+        table_scales = sb.tile([P, J], U8, align_bytes=MX_ALIGN)
+        halves = (slice(0, HALF), slice(HALF, J))
+        for cols in halves:
+            quantise(table_codes[:, cols], table_scales[:, cols], table[:, cols, :].rearrange("p j r -> p (j r)"))
 
-        value_woven, value_codes, value_scales, whole, banks, turned_banks = {}, {}, {}, {}, {}, {}
+        turned, value_codes, value_scales, sums, whole = {}, {}, {}, {}, {}
 
-        def turn(b, picked, turned, scalar_share):
-            cut = scalar_share // 16
-            if scalar_share > 0:
-                nc.scalar.activation(picked[:, :scalar_share], value_pool[b][:].indirect(token_list[:, :cut]), COPY)
-            if scalar_share < I:
-                nc.vector.tensor_copy(picked[:, scalar_share:], value_pool[b][:].indirect(token_list[:, cut:]))
+        def turn(b, picked, bank_tag, bank_bufs):
             pairs = picked[:].bitcast(F32)
+            turned[b] = psum.tile([P, 2, P], F32, name="turned%d" % b, tag=bank_tag, bufs=bank_bufs)
             for u in range(2):
-                nc.tensor.transpose(turned[:, u, :], pairs[:, u : I // 2 : 2], identity[:])
-            turned_banks[b] = turned
+                nc.tensor.transpose(turned[b][:, u, :], pairs[:, u : I // 2 : 2], identity[:])
 
-        def weave(b, woven):
-            value_woven[b] = woven
+        def pick_on_scalar(b, picked_tag, bank_tag, bank_bufs):
+            picked = on_buffer([P, I], BF16, "picked%d" % b, picked_tag)
+            nc.scalar.activation(picked[:], value_pool[b][:].indirect(token_list[:]), COPY)
+            turn(b, picked, bank_tag, bank_bufs)
+
+        def quantise_values(b, woven_tag, codes_tag):
+            woven = on_buffer([P, P * PACK], BF16, "value_woven%d" % b, woven_tag)
             nc.scalar.copy(
-                woven[:].bitcast(F32).rearrange("p (e u) -> p e u", u=2), turned_banks[b][:].rearrange("p u e -> p e u")
+                woven[:].bitcast(F32).rearrange("p (e u) -> p e u", u=2), turned[b][:].rearrange("p u e -> p e u")
             )
+            value_codes[b] = on_buffer([P, P], U32, "value_codes%d" % b, codes_tag)
+            value_scales[b] = sb.tile([P, P], U8, name="value_scales%d" % b, align_bytes=MX_ALIGN)
+            quantise(value_codes[b][:], value_scales[b][:], woven[:])
 
-        def quantise(b, codes):
-            value_codes[b] = codes
-            value_scales[b] = sb.tile([P, P], U8, name="value_scales%d" % b, align_bytes=64)
-            nc.vector.quantize_mx(out=codes[:].bitcast(FP8X4), scales=value_scales[b][:], in_=value_woven[b][:])
+        def multiply(b):
+            sums[b] = psum.tile([P, J], F32, name="sums%d" % b, tag="raw", bufs=RAW_BANKS)
+            product(sums[b][:], value_codes[b][:], value_scales[b][:], table_codes[:], table_scales[:])
 
-        def multiply(b, bank, window):
-            sums = psum.tile([P, J], F32, name="sums", tag=bank, bufs=1)
-            nc.tensor.matmul_mx(
-                out=sums[:],
-                lhsT=value_codes[b][:].bitcast(FP8X4),
-                lhsT_scale=value_scales[b][:],
-                rhs=table_codes[:].bitcast(FP8X4),
-                rhs_scale=table_scales[:],
-                start=True,
-                stop=True,
-            )
-            banks[b] = sums
-            if window is not None:
-                copy_out(b, window)
+        def copy_out(b, copy, whole_tag):
+            whole[b] = on_buffer([P, J], F32, "whole%d" % b, whole_tag)
+            copy(whole[b][:], sums[b][:])
 
-        def copy_out(b, window):
-            whole[b] = window
-            if b == 0:
-                nc.vector.tensor_copy(window[:], banks[b][:])
-            else:
-                nc.scalar.copy(window[:], banks[b][:])
-
-        def give_out(b, result):
+        def give_out(b, result_tag):
+            result = on_buffer([P, C], F32, "result%d" % b, result_tag)
             nc.vector.tensor_tensor(result[:], whole[b][:].indirect(column_list[:]), gain[:], MULT)
             nc.sync.dma_start(out[b * P : (b + 1) * P, :], result[:])
 
-        def turned_on(tag, bufs):
-            return psum.tile([P, 2, P], F32, name="turned", tag=tag, bufs=bufs)
-
-        def woven_on(b):
-            return sb.tile([P, P * PACK], BF16, name="woven%d" % b, tag="woven%d" % b, align_bytes=64)
-
-        def codes_on(b, tag):
-            return sb.tile([P, P], U32, name="value_codes%d" % b, tag=tag, align_bytes=64)
-
-
-        turn(0, last.tile([P, I], BF16, name="picked0", offset=NOTES_AT), turned_on("raw", 4), I)
-        weave(0, woven_on(0))
-        quantise(0, codes_on(0, "table"))
-        multiply(0, "bank_a", None)
-        turn(1, sb.tile([P, I], BF16, name="picked1"), turned_on("bank_b", 1), I)
-        turn(2, sb.tile([P, I], BF16, name="picked2", tag="woven0", align_bytes=64), turned_on("bank_c", 1), I // 2)
-        weave(1, last.tile([P, P * PACK], BF16, name="woven1", offset=THIRD_AT + 4096, align_bytes=64))
-        weave(2, woven_on(2))
-        copy_out(0, last.tile([P, J], F32, name="whole0", offset=THIRD_AT))
-        quantise(1, last.tile([P, P], U32, name="value_codes1", offset=THIRD_AT + 2048, align_bytes=64))
-        give_out(0, sb.tile([P, C], F32, name="result0"))
-        multiply(1, "bank_b", None)
-        turn(3, sb.tile([P, I], BF16, name="picked3", tag="woven0", align_bytes=64), turned_on("bank_c", 1), LAST_SPLIT)
-        copy_out(1, last.tile([P, J], F32, name="whole1", offset=0))
-        weave(3, last.tile([P, P * PACK], BF16, name="woven3", offset=WOVEN_AT + 1536, align_bytes=64))
-        quantise(2, last.tile([P, P], U32, name="value_codes2", offset=2048, align_bytes=64))
-        quantise(3, codes_on(3, "value_codes3"))
-        multiply(2, "bank_a", last.tile([P, J], F32, name="whole2", offset=WOVEN_AT))
-        multiply(3, "bank_d", sb.tile([P, J], F32, name="whole3"))
-        give_out(1, last.tile([P, C], F32, name="result1", offset=WOVEN_AT + 2048))
-        give_out(2, sb.tile([P, C], F32, name="result2"))
-        give_out(3, sb.tile([P, C], F32, name="result3"))
+        pick_on_scalar(0, "picked_first", "raw", RAW_BANKS)
+        pick_on_scalar(1, "picked_next", "turned", 2)
+        quantise_values(0, "value_pool1", "table")
+        quantise_values(1, "value_woven1", "value_codes1")
+        multiply(0)
+        multiply(1)
+        pick_on_scalar(2, "picked_next", "turned", 2)
+        copy_out(0, nc.vector.tensor_copy, "value_woven1")
+        copy_out(1, nc.scalar.copy, "value_pool2")
+        give_out(0, "result0")
+        picked_last = sb.tile([P, I], BF16)
+        nc.scalar.activation(picked_last[:, :HALF], value_pool[3][:].indirect(token_list[:, : HALF // GROUP]), COPY)
+        nc.vector.tensor_copy(picked_last[:, HALF:], value_pool[3][:].indirect(token_list[:, HALF // GROUP :]))
+        turn(3, picked_last, "turned", 2)
+        quantise_values(2, "value_pool3", "value_codes2")
+        give_out(1, "value_pool3")
+        quantise_values(3, "value_woven3", "value_codes3")
+        multiply(2)
+        copy_out(2, nc.scalar.copy, "whole2")
+        whole[3] = on_buffer([P, J], F32, "whole3", "whole3")
+        for cols in halves:
+            half_sums = psum.tile([P, HALF], F32, tag="half_sums", bufs=2)
+            product(half_sums[:], value_codes[3][:], value_scales[3][:], table_codes[:, cols], table_scales[:, cols])
+            nc.scalar.copy(whole[3][:, cols], half_sums[:])
+        give_out(2, "result2")
+        give_out(3, "result3")

@@ -65,12 +65,12 @@ def tile_attend_tab_plain_picked_kernel(tc, keys_words, keys_scales, notes, rowf
 
         note_planes = notes.rearrange("(p t) u -> p t u", t=PACK)
         nc.sync.dma_start(gain_pairs[:], pgain.rearrange("o (p t) -> (o p) t", t=2))
-        nc.sync.dma_start(note_pool[0][:], note_planes[:, 0, :])
         for h in range(2):
-            nc.scalar.dma_start(
+            nc.sync.dma_start(
                 scale_rows[64 * h : 64 * h + 4, :, :].bitcast(I32),
                 keys_scales[0, 8 * h : 8 * h + 8, :].rearrange("(q r) c -> r q c", r=4).bitcast(I32),
             )
+        nc.sync.dma_start(note_pool[0][:], note_planes[:, 0, :])
         nc.sync.dma_start(note_list[:], offs2)
         nc.sync.dma_start(token_list[:], offs)
         for t in range(1, PACK):

@@ -22,6 +22,7 @@ PACK = 4
 GROUP = 16
 MX_ALIGN = 64
 HALF = 256
+TAIL_STEP = 4 * J
 RAW_BANKS = J // P
 
 
@@ -29,10 +30,14 @@ def tile_attend_tab_plain_picked_kernel(tc, keys_words, keys_scales, notes, rowf
     nc = tc.nc
     with ExitStack() as ctx:
         sb = ctx.enter_context(tc.tile_pool(name="sb", bufs=1))
+        tail = ctx.enter_context(tc.tile_pool(name="tail", bufs=1))
         psum = ctx.enter_context(tc.psum_pool(name="psum", bufs=1))
 
         def on_buffer(shape, dtype, name, tag):
             return sb.tile(shape, dtype, name=name, tag=tag, align_bytes=MX_ALIGN)
+
+        def on_last_pool(shape, dtype, name, place):
+            return tail.tile(shape, dtype, name=name, offset=place * TAIL_STEP, align_bytes=MX_ALIGN)
 
         def quantise(codes, scales, woven):
             nc.vector.quantize_mx(out=codes.bitcast(FP8X4), scales=scales, in_=woven)
@@ -55,7 +60,8 @@ def tile_attend_tab_plain_picked_kernel(tc, keys_words, keys_scales, notes, rowf
         scale_rows = sb.tile([P, 2, T], U8)
         scale_pool = sb.tile([P, T], U8)
         note_pool = [sb.tile([P, U], F32, name="note_pool%d" % t) for t in range(PACK)]
-        value_pool = [on_buffer([P, T], F32, "value_pool%d" % b, "value_pool%d" % b) for b in range(E // P)]
+        value_pool = [on_buffer([P, T], F32, "value_pool%d" % b, "value_pool%d" % b) for b in range(E // P - 1)]
+        value_pool.append(tail.tile([P, T], F32, name="value_pool3", offset=0))
         row_factor = sb.tile([P, PACK], F32)
         gain_pairs = on_buffer([P, 2], F32, "gain_pairs", "picked_first")
         identity = sb.tile([P, P], F32)
@@ -142,7 +148,7 @@ def tile_attend_tab_plain_picked_kernel(tc, keys_words, keys_scales, notes, rowf
         for cols in halves:
             quantise(table_codes[:, cols], table_scales[:, cols], table[:, cols, :].rearrange("p j r -> p (j r)"))
 
-        turned, value_codes, value_scales, sums, whole = {}, {}, {}, {}, {}
+        turned, woven, value_codes, value_scales, sums, whole = {}, {}, {}, {}, {}, {}
 
         def turn(b, picked, bank_tag, bank_bufs):
             pairs = picked[:].bitcast(F32)
@@ -155,51 +161,59 @@ def tile_attend_tab_plain_picked_kernel(tc, keys_words, keys_scales, notes, rowf
             nc.scalar.activation(picked[:], value_pool[b][:].indirect(token_list[:]), COPY)
             turn(b, picked, bank_tag, bank_bufs)
 
-        def quantise_values(b, woven_tag, codes_tag):
-            woven = on_buffer([P, P * PACK], BF16, "value_woven%d" % b, woven_tag)
+        def pick_on_both(b, picked_tag):
+            picked = on_buffer([P, I], BF16, "picked%d" % b, picked_tag)
+            nc.scalar.activation(picked[:, :HALF], value_pool[b][:].indirect(token_list[:, : HALF // GROUP]), COPY)
+            nc.vector.tensor_copy(picked[:, HALF:], value_pool[b][:].indirect(token_list[:, HALF // GROUP :]))
+            turn(b, picked, "turned", 2)
+
+        def weave(b, woven_tag):
+            woven[b] = on_buffer([P, P * PACK], BF16, "value_woven%d" % b, woven_tag)
             nc.scalar.copy(
-                woven[:].bitcast(F32).rearrange("p (e u) -> p e u", u=2), turned[b][:].rearrange("p u e -> p e u")
+                woven[b][:].bitcast(F32).rearrange("p (e u) -> p e u", u=2), turned[b][:].rearrange("p u e -> p e u")
             )
-            value_codes[b] = on_buffer([P, P], U32, "value_codes%d" % b, codes_tag)
+
+        def quantise_values(b, codes):
+            value_codes[b] = codes
             value_scales[b] = sb.tile([P, P], U8, name="value_scales%d" % b, align_bytes=MX_ALIGN)
-            quantise(value_codes[b][:], value_scales[b][:], woven[:])
+            quantise(codes[:], value_scales[b][:], woven[b][:])
 
         def multiply(b):
             sums[b] = psum.tile([P, J], F32, name="sums%d" % b, tag="raw", bufs=RAW_BANKS)
             product(sums[b][:], value_codes[b][:], value_scales[b][:], table_codes[:], table_scales[:])
 
-        def copy_out(b, copy, whole_tag):
-            whole[b] = on_buffer([P, J], F32, "whole%d" % b, whole_tag)
-            copy(whole[b][:], sums[b][:])
+        def copy_out(b, copy, window):
+            whole[b] = window
+            copy(window[:], sums[b][:])
 
-        def give_out(b, result_tag):
-            result = on_buffer([P, C], F32, "result%d" % b, result_tag)
+        def give_out(b, result):
             nc.vector.tensor_tensor(result[:], whole[b][:].indirect(column_list[:]), gain[:], MULT)
             nc.sync.dma_start(out[b * P : (b + 1) * P, :], result[:])
 
         pick_on_scalar(0, "picked_first", "raw", RAW_BANKS)
-        pick_on_scalar(1, "picked_next", "turned", 2)
-        quantise_values(0, "value_pool1", "table")
-        quantise_values(1, "value_woven1", "value_codes1")
+        weave(0, "value_woven0")
+        quantise_values(0, on_buffer([P, P], U32, "value_codes0", "table"))
         multiply(0)
+        pick_on_scalar(1, "picked1", "turned", 2)
+        pick_on_both(2, "value_woven0")
+        weave(1, "value_pool2")
+        weave(2, "value_woven2")
+        quantise_values(1, sb.tile([P, P], U32, name="value_codes1", align_bytes=MX_ALIGN))
+        copy_out(0, nc.vector.tensor_copy, on_buffer([P, J], F32, "whole0", "value_pool2"))
         multiply(1)
-        pick_on_scalar(2, "picked_next", "turned", 2)
-        copy_out(0, nc.vector.tensor_copy, "value_woven1")
-        copy_out(1, nc.scalar.copy, "value_pool2")
-        give_out(0, "result0")
-        picked_last = sb.tile([P, I], BF16)
-        nc.scalar.activation(picked_last[:, :HALF], value_pool[3][:].indirect(token_list[:, : HALF // GROUP]), COPY)
-        nc.vector.tensor_copy(picked_last[:, HALF:], value_pool[3][:].indirect(token_list[:, HALF // GROUP :]))
-        turn(3, picked_last, "turned", 2)
-        quantise_values(2, "value_pool3", "value_codes2")
-        give_out(1, "value_pool3")
-        quantise_values(3, "value_woven3", "value_codes3")
+        pick_on_both(3, "value_woven0")
+        copy_out(1, nc.scalar.copy, on_last_pool([P, J], F32, "whole1", 0))
+        weave(3, "value_woven3")
+        quantise_values(2, on_last_pool([P, P], U32, "value_codes2", 1))
+        give_out(0, on_last_pool([P, C], F32, "result0", 2))
+        quantise_values(3, sb.tile([P, P], U32, name="value_codes3", align_bytes=MX_ALIGN))
         multiply(2)
-        copy_out(2, nc.scalar.copy, "whole2")
-        whole[3] = on_buffer([P, J], F32, "whole3", "whole3")
+        copy_out(2, nc.scalar.copy, sb.tile([P, J], F32, name="whole2"))
+        whole[3] = sb.tile([P, J], F32, name="whole3")
         for cols in halves:
             half_sums = psum.tile([P, HALF], F32, tag="half_sums", bufs=2)
             product(half_sums[:], value_codes[3][:], value_scales[3][:], table_codes[:, cols], table_scales[:, cols])
             nc.scalar.copy(whole[3][:, cols], half_sums[:])
-        give_out(2, "result2")
-        give_out(3, "result3")
+        give_out(1, on_buffer([P, C], F32, "result1", "value_woven3"))
+        give_out(2, sb.tile([P, C], F32, name="result2"))
+        give_out(3, sb.tile([P, C], F32, name="result3"))

from contextlib import ExitStack

import concourse.mybir as mybir
from concourse.masks import make_identity

D, T, I, J, U, E, C = 512, 2048, 512, 512, 1024, 512, 256
FLOPS = 2 * D * I * J + 2 * I * E * J

F32 = mybir.dt.float32
BF16 = mybir.dt.bfloat16
I32 = mybir.dt.int32
U32 = mybir.dt.uint32
U16 = mybir.dt.uint16
U8 = mybir.dt.uint8
FP8X4 = mybir.dt.float8_e4m3fn_x4
COPY = mybir.ActivationFunctionType.Copy
MULT = mybir.AluOpType.mult
MAX = mybir.AluOpType.max

P = 128
PACK = 4
GROUP = 16
MX_ALIGN = 64
HALF = 256
TAIL_STEP = 4 * J
RAW_BANKS = J // P


def tile_attend_tab_plain_picked_kernel(tc, keys_words, keys_scales, notes, rowf, vals, pgain, offs, offs2, offs3, out):
    nc = tc.nc
    with ExitStack() as ctx:
        sb = ctx.enter_context(tc.tile_pool(name="sb", bufs=1))
        tail = ctx.enter_context(tc.tile_pool(name="tail", bufs=1))
        psum = ctx.enter_context(tc.psum_pool(name="psum", bufs=1))

        def on_buffer(shape, dtype, name, tag):
            return sb.tile(shape, dtype, name=name, tag=tag, align_bytes=MX_ALIGN)

        def on_last_pool(shape, dtype, name, place):
            return tail.tile(shape, dtype, name=name, offset=place * TAIL_STEP, align_bytes=MX_ALIGN)

        def quantise(codes, scales, woven):
            nc.vector.quantize_mx(out=codes.bitcast(FP8X4), scales=scales, in_=woven)

        def product(sums, lhs_codes, lhs_scales, rhs_codes, rhs_scales):
            nc.tensor.matmul_mx(
                out=sums,
                lhsT=lhs_codes.bitcast(FP8X4),
                lhsT_scale=lhs_scales,
                rhs=rhs_codes.bitcast(FP8X4),
                rhs_scale=rhs_scales,
                start=True,
                stop=True,
            )

        token_list = sb.tile([P, I // GROUP], U16)
        note_list = sb.tile([P, J // GROUP], U16)
        column_list = sb.tile([P, C // GROUP], U16)
        key_pool = on_buffer([P, T], U32, "key_pool", "key_pool")
        scale_rows = sb.tile([P, 2, T], U8)
        scale_pool = sb.tile([P, T], U8)
        note_pool = [sb.tile([P, U], F32, name="note_pool%d" % t) for t in range(PACK)]
        value_pool = [on_buffer([P, T], F32, "value_pool%d" % b, "value_pool%d" % b) for b in range(E // P - 1)]
        value_pool.append(tail.tile([P, T], F32, name="value_pool3", offset=0))
        row_factor = sb.tile([P, PACK], F32)
        gain_pairs = on_buffer([P, 2], F32, "gain_pairs", "picked_first")
        identity = sb.tile([P, P], F32)

        make_identity(nc, identity[:])
        nc.vector.memset(scale_pool[:].bitcast(I32), 0)

        note_planes = notes.rearrange("(p t) u -> p t u", t=PACK)
        nc.sync.dma_start(gain_pairs[:], pgain.rearrange("o (p t) -> (o p) t", t=2))
        for h in range(2):
            nc.sync.dma_start(
                scale_rows[64 * h : 64 * h + 4, :, :].bitcast(I32),
                keys_scales[0, 8 * h : 8 * h + 8, :].rearrange("(q r) c -> r q c", r=4).bitcast(I32),
            )
        nc.sync.dma_start(note_pool[0][:], note_planes[:, 0, :])
        nc.sync.dma_start(note_list[:], offs2)
        nc.sync.dma_start(token_list[:], offs)
        for t in range(1, PACK):
            nc.sync.dma_start(note_pool[t][:], note_planes[:, t, :])
        nc.sync.dma_start(key_pool[:].bitcast(I32), keys_words[0].rearrange("p n t -> p (n t)").bitcast(I32))
        nc.sync.dma_start(row_factor[:], rowf.rearrange("(p t) o -> p (t o)", t=PACK))
        nc.sync.dma_start(value_pool[0][:], vals[0:P, :])
        nc.sync.dma_start(column_list[:], offs3)
        for b in range(1, E // P):
            nc.sync.dma_start(value_pool[b][:], vals[b * P : (b + 1) * P, :])

        gain_turned = psum.tile([P, 2, P], F32, tag="turned", bufs=2)
        for t in range(2):
            nc.tensor.transpose(gain_turned[:, t, :], gain_pairs[:, t : t + 1].to_broadcast([P, P]), identity[:])
        gain = sb.tile([P, C], F32)
        nc.scalar.copy(gain[:].rearrange("p (k t) -> p k t", t=2), gain_turned[:].rearrange("p t k -> p k t"))

        for q in range(4):
            h, pair = divmod(q, 2)
            nc.vector.tensor_copy(
                scale_pool[32 * q : 32 * q + 4, :].bitcast(I32), scale_rows[64 * h : 64 * h + 4, pair, :].bitcast(I32)
            )
        key_scales = sb.tile([P, I], U8, align_bytes=MX_ALIGN)
        nc.vector.tensor_copy(
            key_scales[:].rearrange("p (r s) -> p s r", r=PACK), scale_pool[:].indirect(token_list[:])
        )

        note_picked = on_buffer([P, PACK, J], BF16, "note_picked", "picked_first")
        for t in range(2):
            nc.scalar.activation(note_picked[:, t, :], note_pool[t][:].indirect(note_list[:]), COPY)
        nc.vector.tensor_copy(note_picked[:, 2, :], note_pool[2][:].indirect(note_list[:]))
        nc.vector.tensor_copy(note_picked[:, 3, :HALF], note_pool[3][:].indirect(note_list[:, : HALF // GROUP]))
        nc.scalar.activation(note_picked[:, 3, HALF:], note_pool[3][:].indirect(note_list[:, HALF // GROUP :]), COPY)

        note_woven = [on_buffer([P, HALF, PACK], BF16, "note_woven%d" % h, "note_woven%d" % h) for h in range(2)]
        for h, copy in enumerate((nc.vector.tensor_copy, nc.scalar.copy)):
            copy(
                note_woven[h][:].rearrange("p (c i) t -> p c t i", i=4),
                note_picked[:, :, h * HALF : (h + 1) * HALF].rearrange("p t (c i) -> p c t i", i=4),
            )

        note_scales = [sb.tile([P, HALF], U8, name="note_scales%d" % h, align_bytes=MX_ALIGN) for h in range(2)]
        note_codes = [sb.tile([P, HALF], U32, name="note_codes0", align_bytes=MX_ALIGN)]
        quantise(note_codes[0][:], note_scales[0][:], note_woven[0][:].rearrange("p j t -> p (j t)"))
        key_codes = on_buffer([P, I], U32, "key_codes", "note_woven0")
        nc.vector.tensor_copy(key_codes[:].rearrange("p (r s) -> p s r", r=PACK), key_pool[:].indirect(token_list[:]))
        note_codes.append(on_buffer([P, HALF], U32, "note_codes1", "key_pool"))
        quantise(note_codes[1][:], note_scales[1][:], note_woven[1][:].rearrange("p j t -> p (j t)"))

        table = on_buffer([P, J, PACK], BF16, "table", "table")
        for q in range(RAW_BANKS):
            h, within = divmod(q * P, HALF)
            cols = slice(within, within + P)
            raw = psum.tile([P, PACK, P], F32, tag="raw", bufs=RAW_BANKS)
            for r in range(PACK):
                rows = slice(r * P, (r + 1) * P)
                product(raw[:, r, :], key_codes[:, rows], key_scales[:, rows], note_codes[h][:, cols], note_scales[h][:, cols])
            nc.vector.scalar_tensor_tensor(
                out=table[:, q * P : (q + 1) * P, :],
                in0=raw[:].rearrange("p r j -> p j r"),
                scalar=0.0,
                in1=row_factor[:].unsqueeze(1).to_broadcast([P, P, PACK]),
                op0=MAX,
                op1=MULT,
            )
        table_codes = sb.tile([P, J], U32, align_bytes=MX_ALIGN)
        table_scales = sb.tile([P, J], U8, align_bytes=MX_ALIGN)
        halves = (slice(0, HALF), slice(HALF, J))
        for cols in halves:
            quantise(table_codes[:, cols], table_scales[:, cols], table[:, cols, :].rearrange("p j r -> p (j r)"))

        turned, woven, value_codes, value_scales, sums, whole = {}, {}, {}, {}, {}, {}

        def turn(b, picked, bank_tag, bank_bufs):
            pairs = picked[:].bitcast(F32)
            turned[b] = psum.tile([P, 2, P], F32, name="turned%d" % b, tag=bank_tag, bufs=bank_bufs)
            for u in range(2):
                nc.tensor.transpose(turned[b][:, u, :], pairs[:, u : I // 2 : 2], identity[:])

        def pick_on_scalar(b, picked_tag, bank_tag, bank_bufs):
            picked = on_buffer([P, I], BF16, "picked%d" % b, picked_tag)
            nc.scalar.activation(picked[:], value_pool[b][:].indirect(token_list[:]), COPY)
            turn(b, picked, bank_tag, bank_bufs)

        def pick_on_both(b, picked_tag):
            picked = on_buffer([P, I], BF16, "picked%d" % b, picked_tag)
            nc.scalar.activation(picked[:, :HALF], value_pool[b][:].indirect(token_list[:, : HALF // GROUP]), COPY)
            nc.vector.tensor_copy(picked[:, HALF:], value_pool[b][:].indirect(token_list[:, HALF // GROUP :]))
            turn(b, picked, "turned", 2)

        def weave(b, woven_tag):
            woven[b] = on_buffer([P, P * PACK], BF16, "value_woven%d" % b, woven_tag)
            nc.scalar.copy(
                woven[b][:].bitcast(F32).rearrange("p (e u) -> p e u", u=2), turned[b][:].rearrange("p u e -> p e u")
            )

        def quantise_values(b, codes):
            value_codes[b] = codes
            value_scales[b] = sb.tile([P, P], U8, name="value_scales%d" % b, align_bytes=MX_ALIGN)
            quantise(codes[:], value_scales[b][:], woven[b][:])

        def multiply(b):
            sums[b] = psum.tile([P, J], F32, name="sums%d" % b, tag="raw", bufs=RAW_BANKS)
            product(sums[b][:], value_codes[b][:], value_scales[b][:], table_codes[:], table_scales[:])

        def copy_out(b, copy, window):
            whole[b] = window
            copy(window[:], sums[b][:])

        def give_out(b, result):
            nc.vector.tensor_tensor(result[:], whole[b][:].indirect(column_list[:]), gain[:], MULT)
            nc.sync.dma_start(out[b * P : (b + 1) * P, :], result[:])

        pick_on_scalar(0, "picked_first", "raw", RAW_BANKS)
        weave(0, "value_woven0")
        quantise_values(0, on_buffer([P, P], U32, "value_codes0", "table"))
        multiply(0)
        pick_on_scalar(1, "picked1", "turned", 2)
        pick_on_both(2, "value_woven0")
        weave(1, "value_pool2")
        weave(2, "value_woven2")
        quantise_values(1, sb.tile([P, P], U32, name="value_codes1", align_bytes=MX_ALIGN))
        copy_out(0, nc.vector.tensor_copy, on_buffer([P, J], F32, "whole0", "value_pool2"))
        multiply(1)
        pick_on_both(3, "value_woven0")
        copy_out(1, nc.scalar.copy, on_last_pool([P, J], F32, "whole1", 0))
        weave(3, "value_woven3")
        quantise_values(2, on_last_pool([P, P], U32, "value_codes2", 1))
        give_out(0, on_last_pool([P, C], F32, "result0", 2))
        quantise_values(3, sb.tile([P, P], U32, name="value_codes3", align_bytes=MX_ALIGN))
        multiply(2)
        copy_out(2, nc.scalar.copy, sb.tile([P, J], F32, name="whole2"))
        whole[3] = sb.tile([P, J], F32, name="whole3")
        for cols in halves:
            half_sums = psum.tile([P, HALF], F32, tag="half_sums", bufs=2)
            product(half_sums[:], value_codes[3][:], value_scales[3][:], table_codes[:, cols], table_scales[:, cols])
            nc.scalar.copy(whole[3][:, cols], half_sums[:])
        give_out(1, on_buffer([P, C], F32, "result1", "value_woven3"))
        give_out(2, sb.tile([P, C], F32, name="result2"))
        give_out(3, sb.tile([P, C], F32, name="result3"))
